import numpy as np
import ml_dtypes


def mxq(x, axis, fmt="e4m3"):
    dtype, down = {"e4m3": (ml_dtypes.float8_e4m3fn, 7), "e5m2": (ml_dtypes.float8_e5m2, 14)}[fmt]
    v = np.moveaxis(np.asarray(x, np.float32).astype(ml_dtypes.bfloat16).astype(np.float64), axis, -1)
    blocks = v.reshape(v.shape[:-1] + (-1, 32))
    amax = np.abs(blocks).max(-1, keepdims=True)
    byte = np.maximum(np.where(amax > 0, np.frexp(amax)[1] - 1 + 127, 0) - down, 1)
    scale = np.exp2(byte - 127.0)
    codes = (blocks / scale).astype(np.float32).astype(dtype).astype(np.float64)
    return np.moveaxis((codes * scale).reshape(v.shape), -1, axis)


WIDE = False


def mx_kscale(k):
    if not WIDE:
        return np.ones(k)
    levels = np.array([10, -10, 5, -5, 0])
    if k % 512:
        return np.exp2(np.random.permutation(np.resize(levels, k // 32))).repeat(32)
    a = np.empty((k // 512, 16))
    for p in range(k // 512):
        a[p, :8] = np.random.permutation(np.resize(levels, 8))
        for g in range(8):
            far = levels[np.abs(levels - a[p, g]) >= 10]
            a[p, g + 8] = far[np.random.randint(len(far))]
    return np.exp2(a.ravel()).repeat(32)


def f64(x):
    return np.asarray(x).astype(np.float64)


def striped(idx):
    return np.tile(np.asarray(idx).reshape(-1, 16).T, (8, 1)).astype(np.uint16)


def unstriped(offs):
    return offs[:16].T.reshape(-1).astype(np.int64)


E2M1 = np.array([0.0, 0.5, 1.0, 1.5, 2.0, 3.0, 4.0, 6.0, -0.0, -0.5, -1.0, -1.5, -2.0, -3.0, -4.0, -6.0])


def pack_weight(w, fmt):
    k, n = w.shape
    w = f64(np.asarray(w, np.float32).astype(ml_dtypes.bfloat16)).reshape(k // 32, 32, n)
    amax = np.abs(w).max(1)
    if fmt == "e4m3":
        byte = np.frexp(amax)[1] - 1 + 127 - 7
    else:
        mant, ex = np.frexp(amax / 6.0)
        byte = np.where(mant > 0.5, ex, ex - 1) + 127
    byte = np.clip(np.where(amax > 0, byte, 1), 1, 254)
    scaled = (w * np.exp2(127.0 - byte)[:, None, :]).reshape(k, n).astype(np.float32)
    by_word = np.ascontiguousarray(scaled.reshape(k // 512, 128, 4, n).transpose(0, 1, 3, 2))
    if fmt == "e4m3":
        words = by_word.astype(ml_dtypes.float8_e4m3fn).view(np.uint8)
    else:
        c = by_word.astype(ml_dtypes.float4_e2m1fn).view(np.uint8) & 0xF
        words = (c[..., 0::2] | (c[..., 1::2] << 4)).reshape(k // 512, 128, 2 * n)
    return np.ascontiguousarray(words), np.ascontiguousarray(byte.astype(np.uint8).reshape(k // 512, 16, n))


def unpack_weight(words, scales, fmt):
    g, _, n = scales.shape
    words = np.ascontiguousarray(words).reshape(g, 128, n, -1)
    if fmt == "e4m3":
        vals = words.view(ml_dtypes.float8_e4m3fn).astype(np.float64)
    else:
        nib = np.empty((g, 128, n, 4), np.uint8)
        nib[..., 0::2] = words & 0xF
        nib[..., 1::2] = words >> 4
        vals = E2M1[nib]
    vals = vals * np.repeat(np.exp2(scales.astype(np.float64) - 127.0), 8, axis=1)[..., None]
    return vals.transpose(0, 1, 3, 2).reshape(g * 512, n)


def softplus(v):
    return np.log(1.0 + np.exp(v))


K, L, T, J, N = 512, 512, 1024, 512, 512


def setup_inputs():
    n = np.random.standard_normal
    idx = np.random.permutation(T)[:J]
    fk = mx_kscale(K)
    fl = mx_kscale(L)
    xap = pack_weight(n((K, J)) / fk[:, None], "e2m1")
    wap = pack_weight(n((K, N)) * 1 / np.sqrt(K) * fk[:, None], "e4m3")
    wbp = pack_weight(n((L, N)) * 1 / np.sqrt(L) * fl[:, None], "e2m1")
    return {
        "xa_words": xap[0],
        "xa_scales": xap[1],
        "wa_words": wap[0],
        "wa_scales": wap[1],
        "xb": (n((L, J)) / fl[:, None]).astype(np.float32),
        "wb_words": wbp[0],
        "wb_scales": wbp[1],
        "pr": (np.random.uniform(0.4, 2.0, (N, T))).astype(np.float32),
        "old": (1.0 * n((N, T))).astype(np.float32),
        "offs": striped(idx),
    }


def reference(xa_words, xa_scales, wa_words, wa_scales, xb, wb_words, wb_scales, pr, old, offs):
    idx = unstriped(offs)
    xau = unpack_weight(xa_words, xa_scales, "e2m1")
    wau = unpack_weight(wa_words, wa_scales, "e4m3")
    wbu = unpack_weight(wb_words, wb_scales, "e2m1")
    v = wau.T @ xau
    xbq = mxq(f64(xb), 0, "e4m3")
    u = wbu.T @ xbq
    s = softplus(u)
    sv = s * v
    num = np.zeros((N, T))
    num[:, idx] = sv
    den = np.zeros((N, T))
    den[:, idx] = s
    y = (num + f64(pr) * f64(old)) / (den + f64(pr))
    return y

@@ -1,0 +1,210 @@
+from contextlib import ExitStack
+
+import concourse.mybir as mybir
+from concourse.masks import make_identity
+
+K, L, T, J, N = 512, 512, 1024, 512, 512
+FLOPS = 2 * K * N * J + 2 * L * N * J
+
+F32 = mybir.dt.float32
+BF16 = mybir.dt.bfloat16
+I32 = mybir.dt.int32
+U32 = mybir.dt.uint32
+U16 = mybir.dt.uint16
+U8 = mybir.dt.uint8
+FP8X4 = mybir.dt.float8_e4m3fn_x4
+FP4X4 = mybir.dt.float4_e2m1fn_x4
+ACT = mybir.ActivationFunctionType
+ALU = mybir.AluOpType
+
+P = 128
+PACK = 4
+TILES = N // P
+BANK = 512
+HEAD = 128
+REST = J - HEAD
+REST_PARTS = ((0, 128), (128, 384))
+
+
+def tile_list_weighted_writes_kernel(tc, xa_words, xa_scales, wa_words, wa_scales, xb, wb_words, wb_scales, pr, old, offs, out):
+    nc = tc.nc
+    with ExitStack() as ctx:
+        sb = ctx.enter_context(tc.tile_pool(name="sb", bufs=1))
+        ring = ctx.enter_context(tc.tile_pool(name="ring", bufs=2))
+        pages = ctx.enter_context(tc.tile_pool(name="pages", bufs=1))
+        psum = ctx.enter_context(tc.psum_pool(name="psum", bufs=1))
+
+        def bank(i, name):
+            return psum.tile([P, BANK], F32, name=name, tag="bank%d" % i)
+
+        def load_scales(plane, rows):
+            for q in range(4):
+                nc.sync.dma_start(out=plane[32 * q : 32 * q + 4, :].bitcast(I32), in_=rows[0, 4 * q : 4 * q + 4, :].bitcast(I32))
+
+        def pair(i, name):
+            return psum.tile([P, 2 * BANK], F32, name=name, tag="pair%d" % i)
+
+        xb_rows = xb.rearrange("(p r) j -> p r j", r=PACK)
+        raw_head = pages.tile([P, PACK, 6 * T // PACK], F32, name="raw_head", offset=2 * 4 * T)
+        raw_rest = sb.tile([P, PACK, REST], F32, name="raw_rest")
+        wb_codes = sb.tile([P, 2 * N], U8, name="wb_codes", align_bytes=64)
+        wb_plane = sb.tile([P, N], U8, name="wb_plane", align_bytes=64)
+        xa_codes = sb.tile([P, 2 * J], U8, name="xa_codes", align_bytes=64)
+        xa_plane = sb.tile([P, J], U8, name="xa_plane", align_bytes=64)
+        wa_codes = sb.tile([P, N], U32, name="wa_codes", align_bytes=64)
+        wa_plane = sb.tile([P, N], U8, name="wa_plane", align_bytes=64)
+        offsets = sb.tile([P, J // 16], U16, name="offsets")
+
+        for plane in (wb_plane, wa_plane, xa_plane):
+            nc.vector.memset(plane[:].bitcast(U32), 0)
+
+        nc.sync.dma_start(out=raw_head[:, :, 0:HEAD], in_=xb_rows[:, :, 0:HEAD])
+        load_scales(wb_plane, wb_scales)
+        nc.sync.dma_start(out=wb_codes[:].bitcast(I32), in_=wb_words[0].bitcast(I32))
+        nc.sync.dma_start(out=raw_rest[:], in_=xb_rows[:, :, HEAD:J])
+        nc.sync.dma_start(offsets[:], offs)
+        load_scales(wa_plane, wa_scales)
+        load_scales(xa_plane, xa_scales)
+        nc.sync.dma_start(out=xa_codes[:].bitcast(I32), in_=xa_words[0].bitcast(I32))
+        nc.sync.dma_start(out=wa_codes[:].bitcast(I32), in_=wa_words[0].rearrange("p n r -> p (n r)").bitcast(I32))
+        prior, state = [], []
+        for t in range(TILES):
+            prior.append(sb.tile([P, T], F32, name="prior%d" % t))
+            state.append(sb.tile([P, T], F32, name="state%d" % t))
+            nc.sync.dma_start(out=prior[t][:], in_=pr[P * t : P * (t + 1), :])
+            nc.sync.dma_start(out=state[t][:], in_=old[P * t : P * (t + 1), :])
+
+        ident = sb.tile([P, P], F32, name="ident")
+        make_identity(nc, ident[:])
+
+        xb_codes = sb.tile([P, J], U32, name="xb_codes", align_bytes=64)
+        xb_plane = sb.tile([P, J], U8, name="xb_plane", align_bytes=64)
+
+        def interleave(raw, lo, hi, name):
+            grouped = sb.tile([P, (hi - lo) * PACK], BF16, name=name, align_bytes=64)
+            nc.vector.tensor_copy(
+                out=grouped[:].rearrange("p (c i r) -> p c r i", i=4, r=PACK),
+                in_=raw[:, :, lo:hi].rearrange("p r (c i) -> p c r i", i=4),
+            )
+            return grouped
+
+        def quantise(grouped, j0, j1):
+            nc.vector.quantize_mx(out=xb_codes[:, j0:j1].bitcast(FP8X4), scales=xb_plane[:, j0:j1], in_=grouped[:])
+
+        def product_u(dst, t, j0, j1):
+            nc.tensor.matmul_mx(
+                dst,
+                lhsT=wb_codes[:, 2 * P * t : 2 * P * (t + 1)].bitcast(FP4X4),
+                lhsT_scale=wb_plane[:, P * t : P * (t + 1)],
+                rhs=xb_codes[:, j0:j1].bitcast(FP8X4),
+                rhs_scale=xb_plane[:, j0:j1],
+                start=True,
+                stop=True,
+            )
+
+        def product_v(dst, t, j0, j1):
+            nc.tensor.matmul_mx(
+                dst,
+                lhsT=wa_codes[:, P * t : P * (t + 1)].bitcast(FP8X4),
+                lhsT_scale=wa_plane[:, P * t : P * (t + 1)],
+                rhs=xa_codes[:, 2 * j0 : 2 * j1].bitcast(FP4X4),
+                rhs_scale=xa_plane[:, j0:j1],
+                start=True,
+                stop=True,
+            )
+
+        quantise(interleave(raw_head, 0, HEAD, "grouped_head"), 0, HEAD)
+        u_head = bank(0, "u_head")
+        for t in range(TILES):
+            product_u(u_head[:, HEAD * t : HEAD * (t + 1)], t, 0, HEAD)
+        decay = sb.tile([P, TILES, REST], F32, name="decay")
+        log_head = sb.tile([P, TILES, HEAD], F32, name="log_head")
+        nc.scalar.activation(decay[:, :, 0:HEAD], u_head[:].rearrange("p (t j) -> p t j", t=TILES), ACT.Abs)
+        nc.scalar.activation(decay[:, :, 0:HEAD], decay[:, :, 0:HEAD], ACT.Exp, scale=-1.0)
+        nc.scalar.activation(log_head[:], decay[:, :, 0:HEAD], ACT.Ln, bias=1.0)
+
+        grouped = [interleave(raw_rest, lo, hi, "grouped%d" % lo) for lo, hi in REST_PARTS]
+        for g, (lo, hi) in zip(grouped, REST_PARTS):
+            quantise(g, HEAD + lo, HEAD + hi)
+        uv = [pair(t, "uv%d" % t) for t in range(2)]
+        u_rest = [uv[0][:, 0:BANK], uv[1][:, 0:BANK], bank(2, "u_rest2"), bank(3, "u_rest3")]
+        for t in range(TILES):
+            for lo, hi in REST_PARTS:
+                product_u(u_rest[t][:, lo:hi], t, HEAD + lo, HEAD + hi)
+        v_head = bank(1, "v_head")
+        for t in range(TILES):
+            product_v(v_head[:, HEAD * t : HEAD * (t + 1)], t, 0, HEAD)
+
+        den, num = [], []
+        for t in range(TILES):
+            den.append(pages.tile([P, T], F32, name="den%d" % t, offset=4 * T * t))
+            num.append(pages.tile([P, T], F32, name="num%d" % t, offset=4 * T * (TILES + t)))
+        for page in den + num:
+            nc.vector.memset(page[:], 0.0)
+
+        s_head = sb.tile([P, TILES * HEAD], F32, name="s_head")
+        sv_head = sb.tile([P, TILES * HEAD], F32, name="sv_head")
+        nc.vector.scalar_tensor_tensor(s_head[:], u_head[:], 0.0, log_head[:].rearrange("p t j -> p (t j)"), ALU.max, ALU.add)
+        nc.vector.tensor_tensor(sv_head[:], s_head[:], v_head[:], ALU.mult)
+        head_list = offsets[:, 0 : HEAD // 16]
+        for t in range(TILES):
+            nc.vector.tensor_copy(den[t][:].indirect(head_list), s_head[:, HEAD * t : HEAD * (t + 1)])
+        for t in range(TILES):
+            nc.vector.tensor_copy(num[t][:].indirect(head_list), sv_head[:, HEAD * t : HEAD * (t + 1)])
+
+        v_rest = [uv[0][:, BANK : 2 * BANK], uv[1][:, BANK : 2 * BANK], bank(0, "v_rest2"), bank(1, "v_rest3")]
+        for t in range(TILES):
+            for lo, hi in REST_PARTS:
+                product_v(v_rest[t][:, lo:hi], t, HEAD + lo, HEAD + hi)
+
+        for t in range(TILES):
+            nc.scalar.activation(decay[:, t, :], u_rest[t][:, 0:REST], ACT.Abs)
+        nc.scalar.activation(decay[:], decay[:], ACT.Exp, scale=-1.0)
+        log_rest = [sb.tile([P, REST], F32, name="log_rest%d" % t) for t in range(TILES)]
+        for t in range(TILES):
+            nc.scalar.activation(log_rest[t][:], decay[:, t, :], ACT.Ln, bias=1.0)
+
+        weighted = [sb.tile([P, T], F32, name="weighted%d" % t) for t in range(TILES)]
+        for t in range(TILES):
+            nc.gpsimd.tensor_tensor(weighted[t][:], prior[t][:], state[t][:], ALU.mult)
+
+        rest_list = offsets[:, HEAD // 16 : J // 16]
+        for t in range(TILES):
+            s = ring.tile([P, REST], F32, name="s")
+            sv = ring.tile([P, REST], F32, name="sv")
+            nc.vector.scalar_tensor_tensor(s[:], u_rest[t][:, 0:REST], 0.0, log_rest[t][:], ALU.max, ALU.add)
+            nc.vector.tensor_tensor(sv[:], s[:], v_rest[t][:, 0:REST], ALU.mult)
+            nc.vector.tensor_copy(den[t][:].indirect(rest_list), s[:])
+            nc.vector.tensor_copy(num[t][:].indirect(rest_list), sv[:])
+
+            recip = sb.tile([P, T], F32, name="recip%d" % t)
+            halves = [slice(BANK * h, BANK * (h + 1)) for h in range(2)]
+            blocks = [[slice(BANK * h + P * k, BANK * h + P * (k + 1)) for k in range(BANK // P)] for h in range(2)]
+            total = pair(0, "total")
+            for h in range(2):
+                for k, cols in enumerate(blocks[h]):
+                    nc.tensor.matmul(total[:, cols], prior[t][:, cols], ident[:], start=(k == 0), stop=False, is_transpose=True)
+            root = ring.tile([P, T], F32, name="root")
+            for h in range(2):
+                for k, cols in enumerate(blocks[h]):
+                    nc.tensor.matmul(total[:, cols], den[t][:, cols], ident[:], start=False, stop=(k == len(blocks[h]) - 1), is_transpose=True)
+                nc.scalar.activation(root[:, halves[h]], total[:, halves[h]], ACT.Abs_reciprocal_sqrt)
+            back = pair(1, "back")
+            for h in range(2):
+                for cols in blocks[h]:
+                    nc.tensor.transpose(back[:, cols], root[:, cols], ident[:])
+                nc.scalar.activation(recip[:, halves[h]], back[:, halves[h]], ACT.Square)
+
+            rows = slice(P * t, P * (t + 1))
+            result = ring.tile([P, T], F32, name="result")
+            if t < TILES - 1:
+                summed = sb.tile([P, T], F32, name="summed")
+                nc.gpsimd.tensor_tensor(summed[:], num[t][:], weighted[t][:], ALU.add)
+                nc.gpsimd.tensor_tensor(result[:], summed[:], recip[:], ALU.mult)
+                nc.sync.dma_start(out=out[rows, :], in_=result[:])
+            else:
+                for cols in halves:
+                    nc.vector.tensor_tensor(weighted[t][:, cols], num[t][:, cols], weighted[t][:, cols], ALU.add)
+                for cols in halves:
+                    nc.vector.tensor_tensor(result[:, cols], weighted[t][:, cols], recip[:, cols], ALU.mult)
+                    nc.sync.dma_start(out=out[rows, cols], in_=result[:, cols])

@@ -23,6 +23,7 @@ TILES = N // P
 BANK = 512
 HEAD = 128
 REST = J - HEAD
+TINY = 2.0**-60
 REST_PARTS = ((0, 128), (128, 384))
 
 
@@ -45,7 +46,7 @@ def tile_list_weighted_writes_kernel(tc, xa_words, xa_scales, wa_words, wa_scale
             return psum.tile([P, 2 * BANK], F32, name=name, tag="pair%d" % i)
 
         xb_rows = xb.rearrange("(p r) j -> p r j", r=PACK)
-        raw_head = pages.tile([P, PACK, 6 * T // PACK], F32, name="raw_head", offset=2 * 4 * T)
+        raw_head = pages.tile([P, PACK, 2 * T // PACK], F32, name="raw_head", offset=2 * 4 * T)
         raw_rest = sb.tile([P, PACK, REST], F32, name="raw_rest")
         wb_codes = sb.tile([P, 2 * N], U8, name="wb_codes", align_bytes=64)
         wb_plane = sb.tile([P, N], U8, name="wb_plane", align_bytes=64)
@@ -70,7 +71,7 @@ def tile_list_weighted_writes_kernel(tc, xa_words, xa_scales, wa_words, wa_scale
         prior, state = [], []
         for t in range(TILES):
             prior.append(sb.tile([P, T], F32, name="prior%d" % t))
-            state.append(sb.tile([P, T], F32, name="state%d" % t))
+            state.append(sb.tile([P, T], F32, name="state%d" % t, tag="state%d" % t))
             nc.sync.dma_start(out=prior[t][:], in_=pr[P * t : P * (t + 1), :])
             nc.sync.dma_start(out=state[t][:], in_=old[P * t : P * (t + 1), :])
 
@@ -80,16 +81,16 @@ def tile_list_weighted_writes_kernel(tc, xa_words, xa_scales, wa_words, wa_scale
         xb_codes = sb.tile([P, J], U32, name="xb_codes", align_bytes=64)
         xb_plane = sb.tile([P, J], U8, name="xb_plane", align_bytes=64)
 
-        def interleave(raw, lo, hi, name):
-            grouped = sb.tile([P, (hi - lo) * PACK], BF16, name=name, align_bytes=64)
+        def interleave(raw, lo, hi, room):
+            grouped = room[:, 0 : (hi - lo) * PACK]
             nc.vector.tensor_copy(
-                out=grouped[:].rearrange("p (c i r) -> p c r i", i=4, r=PACK),
+                out=grouped.rearrange("p (c i r) -> p c r i", i=4, r=PACK),
                 in_=raw[:, :, lo:hi].rearrange("p r (c i) -> p c r i", i=4),
             )
             return grouped
 
         def quantise(grouped, j0, j1):
-            nc.vector.quantize_mx(out=xb_codes[:, j0:j1].bitcast(FP8X4), scales=xb_plane[:, j0:j1], in_=grouped[:])
+            nc.vector.quantize_mx(out=xb_codes[:, j0:j1].bitcast(FP8X4), scales=xb_plane[:, j0:j1], in_=grouped)
 
         def product_u(dst, t, j0, j1):
             nc.tensor.matmul_mx(
@@ -113,17 +114,21 @@ def tile_list_weighted_writes_kernel(tc, xa_words, xa_scales, wa_words, wa_scale
                 stop=True,
             )
 
-        quantise(interleave(raw_head, 0, HEAD, "grouped_head"), 0, HEAD)
+        room_head = sb.tile([P, HEAD * PACK], BF16, name="room_head", align_bytes=64)
+        quantise(interleave(raw_head, 0, HEAD, room_head), 0, HEAD)
         u_head = bank(0, "u_head")
         for t in range(TILES):
             product_u(u_head[:, HEAD * t : HEAD * (t + 1)], t, 0, HEAD)
         decay = sb.tile([P, TILES, REST], F32, name="decay")
         log_head = sb.tile([P, TILES, HEAD], F32, name="log_head")
-        nc.scalar.activation(decay[:, :, 0:HEAD], u_head[:].rearrange("p (t j) -> p t j", t=TILES), ACT.Abs)
-        nc.scalar.activation(decay[:, :, 0:HEAD], decay[:, :, 0:HEAD], ACT.Exp, scale=-1.0)
-        nc.scalar.activation(log_head[:], decay[:, :, 0:HEAD], ACT.Ln, bias=1.0)
+        nc.scalar.activation(decay[:, :, 0:HEAD], u_head[:].rearrange("p (t j) -> p t j", t=TILES), ACT.Sigmoid, scale=-1.0)
+        nc.scalar.activation(log_head[:], decay[:, :, 0:HEAD], ACT.Ln, bias=TINY)
 
-        grouped = [interleave(raw_rest, lo, hi, "grouped%d" % lo) for lo, hi in REST_PARTS]
+        rooms = [
+            sb.tile([P, HEAD * PACK], BF16, name="room_first", align_bytes=64),
+            pages.tile([P, 2 * TILES * T], BF16, name="room_last", align_bytes=64, offset=4 * T * TILES),
+        ]
+        grouped = [interleave(raw_rest, lo, hi, room) for room, (lo, hi) in zip(rooms, REST_PARTS)]
         for g, (lo, hi) in zip(grouped, REST_PARTS):
             quantise(g, HEAD + lo, HEAD + hi)
         uv = [pair(t, "uv%d" % t) for t in range(2)]
@@ -139,16 +144,18 @@ def tile_list_weighted_writes_kernel(tc, xa_words, xa_scales, wa_words, wa_scale
         for t in range(TILES):
             den.append(pages.tile([P, T], F32, name="den%d" % t, offset=4 * T * t))
             num.append(pages.tile([P, T], F32, name="num%d" % t, offset=4 * T * (TILES + t)))
-        for page in den + num:
+        for page in den:
             nc.vector.memset(page[:], 0.0)
+        for page in num:
+            nc.gpsimd.memset(page[:], 0.0)
 
         s_head = sb.tile([P, TILES * HEAD], F32, name="s_head")
         sv_head = sb.tile([P, TILES * HEAD], F32, name="sv_head")
-        nc.vector.scalar_tensor_tensor(s_head[:], u_head[:], 0.0, log_head[:].rearrange("p t j -> p (t j)"), ALU.max, ALU.add)
-        nc.vector.tensor_tensor(sv_head[:], s_head[:], v_head[:], ALU.mult)
+        nc.vector.scalar_tensor_tensor(s_head[:], log_head[:].rearrange("p t j -> p (t j)"), -1.0, u_head[:], ALU.mult, ALU.max)
         head_list = offsets[:, 0 : HEAD // 16]
         for t in range(TILES):
             nc.vector.tensor_copy(den[t][:].indirect(head_list), s_head[:, HEAD * t : HEAD * (t + 1)])
+        nc.vector.tensor_tensor(sv_head[:], s_head[:], v_head[:], ALU.mult)
         for t in range(TILES):
             nc.vector.tensor_copy(num[t][:].indirect(head_list), sv_head[:, HEAD * t : HEAD * (t + 1)])
 
@@ -158,11 +165,8 @@ def tile_list_weighted_writes_kernel(tc, xa_words, xa_scales, wa_words, wa_scale
                 product_v(v_rest[t][:, lo:hi], t, HEAD + lo, HEAD + hi)
 
         for t in range(TILES):
-            nc.scalar.activation(decay[:, t, :], u_rest[t][:, 0:REST], ACT.Abs)
-        nc.scalar.activation(decay[:], decay[:], ACT.Exp, scale=-1.0)
-        log_rest = [sb.tile([P, REST], F32, name="log_rest%d" % t) for t in range(TILES)]
-        for t in range(TILES):
-            nc.scalar.activation(log_rest[t][:], decay[:, t, :], ACT.Ln, bias=1.0)
+            nc.scalar.activation(decay[:, t, :], u_rest[t][:, 0:REST], ACT.Sigmoid, scale=-1.0)
+        nc.scalar.activation(decay[:], decay[:], ACT.Ln, bias=TINY)
 
         weighted = [sb.tile([P, T], F32, name="weighted%d" % t) for t in range(TILES)]
         for t in range(TILES):
@@ -172,9 +176,9 @@ def tile_list_weighted_writes_kernel(tc, xa_words, xa_scales, wa_words, wa_scale
         for t in range(TILES):
             s = ring.tile([P, REST], F32, name="s")
             sv = ring.tile([P, REST], F32, name="sv")
-            nc.vector.scalar_tensor_tensor(s[:], u_rest[t][:, 0:REST], 0.0, log_rest[t][:], ALU.max, ALU.add)
-            nc.vector.tensor_tensor(sv[:], s[:], v_rest[t][:, 0:REST], ALU.mult)
+            nc.vector.scalar_tensor_tensor(s[:], decay[:, t, :], -1.0, u_rest[t][:, 0:REST], ALU.mult, ALU.max)
             nc.vector.tensor_copy(den[t][:].indirect(rest_list), s[:])
+            nc.vector.tensor_tensor(sv[:], s[:], v_rest[t][:, 0:REST], ALU.mult)
             nc.vector.tensor_copy(num[t][:].indirect(rest_list), sv[:])
 
             recip = sb.tile([P, T], F32, name="recip%d" % t)
@@ -198,7 +202,7 @@ def tile_list_weighted_writes_kernel(tc, xa_words, xa_scales, wa_words, wa_scale
             rows = slice(P * t, P * (t + 1))
             result = ring.tile([P, T], F32, name="result")
             if t < TILES - 1:
-                summed = sb.tile([P, T], F32, name="summed")
+                summed = sb.tile([P, T], F32, name="summed", tag="state%d" % (TILES - 1))
                 nc.gpsimd.tensor_tensor(summed[:], num[t][:], weighted[t][:], ALU.add)
                 nc.gpsimd.tensor_tensor(result[:], summed[:], recip[:], ALU.mult)
                 nc.sync.dma_start(out=out[rows, :], in_=result[:])

@@ -56,9 +56,6 @@ def tile_list_weighted_writes_kernel(tc, xa_words, xa_scales, wa_words, wa_scale
         wa_plane = sb.tile([P, N], U8, name="wa_plane", align_bytes=64)
         offsets = sb.tile([P, J // 16], U16, name="offsets")
 
-        for plane in (wb_plane, wa_plane, xa_plane):
-            nc.vector.memset(plane[:].bitcast(U32), 0)
-
         nc.sync.dma_start(out=raw_head[:, :, 0:HEAD], in_=xb_rows[:, :, 0:HEAD])
         load_scales(wb_plane, wb_scales)
         nc.sync.dma_start(out=wb_codes[:].bitcast(I32), in_=wb_words[0].bitcast(I32))
@@ -131,8 +128,8 @@ def tile_list_weighted_writes_kernel(tc, xa_words, xa_scales, wa_words, wa_scale
         grouped = [interleave(raw_rest, lo, hi, room) for room, (lo, hi) in zip(rooms, REST_PARTS)]
         for g, (lo, hi) in zip(grouped, REST_PARTS):
             quantise(g, HEAD + lo, HEAD + hi)
-        uv = [pair(t, "uv%d" % t) for t in range(2)]
-        u_rest = [uv[0][:, 0:BANK], uv[1][:, 0:BANK], bank(2, "u_rest2"), bank(3, "u_rest3")]
+        u_pairs = [pair(i, "u_pair%d" % i) for i in range(2)]
+        u_rest = [u_pairs[t // 2][:, BANK * (t % 2) : BANK * (t % 2 + 1)] for t in range(TILES)]
         for t in range(TILES):
             for lo, hi in REST_PARTS:
                 product_u(u_rest[t][:, lo:hi], t, HEAD + lo, HEAD + hi)
@@ -150,16 +147,16 @@ def tile_list_weighted_writes_kernel(tc, xa_words, xa_scales, wa_words, wa_scale
             nc.gpsimd.memset(page[:], 0.0)
 
         s_head = sb.tile([P, TILES * HEAD], F32, name="s_head")
-        sv_head = sb.tile([P, TILES * HEAD], F32, name="sv_head")
+        sv = sb.tile([P, TILES, J], F32, name="sv")
         nc.vector.scalar_tensor_tensor(s_head[:], log_head[:].rearrange("p t j -> p (t j)"), -1.0, u_head[:], ALU.mult, ALU.max)
         head_list = offsets[:, 0 : HEAD // 16]
         for t in range(TILES):
             nc.vector.tensor_copy(den[t][:].indirect(head_list), s_head[:, HEAD * t : HEAD * (t + 1)])
-        nc.vector.tensor_tensor(sv_head[:], s_head[:], v_head[:], ALU.mult)
-        for t in range(TILES):
-            nc.vector.tensor_copy(num[t][:].indirect(head_list), sv_head[:, HEAD * t : HEAD * (t + 1)])
+        nc.vector.tensor_tensor(sv[:, :, 0:HEAD], s_head[:].rearrange("p (t j) -> p t j", t=TILES), v_head[:].rearrange("p (t j) -> p t j", t=TILES), ALU.mult)
+        for t in range(TILES - 1):
+            nc.vector.tensor_copy(num[t][:].indirect(head_list), sv[:, t, 0:HEAD])
 
-        v_rest = [uv[0][:, BANK : 2 * BANK], uv[1][:, BANK : 2 * BANK], bank(0, "v_rest2"), bank(1, "v_rest3")]
+        v_rest = [bank(b, "v_rest%d" % b) for b in (2, 3, 0, 1)]
         for t in range(TILES):
             for lo, hi in REST_PARTS:
                 product_v(v_rest[t][:, lo:hi], t, HEAD + lo, HEAD + hi)
@@ -173,13 +170,16 @@ def tile_list_weighted_writes_kernel(tc, xa_words, xa_scales, wa_words, wa_scale
             nc.gpsimd.tensor_tensor(weighted[t][:], prior[t][:], state[t][:], ALU.mult)
 
         rest_list = offsets[:, HEAD // 16 : J // 16]
+        s_rest = [sb.tile([P, REST], F32, name="s_rest%d" % t) for t in range(TILES)]
         for t in range(TILES):
-            s = ring.tile([P, REST], F32, name="s")
-            sv = ring.tile([P, REST], F32, name="sv")
-            nc.vector.scalar_tensor_tensor(s[:], decay[:, t, :], -1.0, u_rest[t][:, 0:REST], ALU.mult, ALU.max)
-            nc.vector.tensor_copy(den[t][:].indirect(rest_list), s[:])
-            nc.vector.tensor_tensor(sv[:], s[:], v_rest[t][:, 0:REST], ALU.mult)
-            nc.vector.tensor_copy(num[t][:].indirect(rest_list), sv[:])
+            nc.vector.scalar_tensor_tensor(s_rest[t][:], decay[:, t, :], -1.0, u_rest[t][:, 0:REST], ALU.mult, ALU.max)
+        for t in range(TILES):
+            nc.vector.tensor_tensor(sv[:, t, HEAD:J], s_rest[t][:], v_rest[t][:, 0:REST], ALU.mult)
+            nc.vector.tensor_copy(den[t][:].indirect(rest_list), s_rest[t][:])
+            if t < TILES - 1:
+                nc.vector.tensor_copy(num[t][:].indirect(rest_list), sv[:, t, HEAD:J])
+            else:
+                nc.vector.tensor_copy(num[t][:].indirect(offsets[:]), sv[:, t, :])
 
             recip = sb.tile([P, T], F32, name="recip%d" % t)
             halves = [slice(BANK * h, BANK * (h + 1)) for h in range(2)]

@@ -20,11 +20,16 @@ ALU = mybir.AluOpType
 P = 128
 PACK = 4
 TILES = N // P
+LAST = TILES - 1
 BANK = 512
+PAGE_BYTES = 4 * T
+GROUP = 16
+
 HEAD = 128
 REST = J - HEAD
-TINY = 2.0**-60
 REST_PARTS = ((0, 128), (128, 384))
+
+TINY = 2.0**-60
 
 
 def tile_list_weighted_writes_kernel(tc, xa_words, xa_scales, wa_words, wa_scales, xb, wb_words, wb_scales, pr, old, offs, out):
@@ -38,15 +43,18 @@ def tile_list_weighted_writes_kernel(tc, xa_words, xa_scales, wa_words, wa_scale
         def bank(i, name):
             return psum.tile([P, BANK], F32, name=name, tag="bank%d" % i)
 
-        def load_scales(plane, rows):
-            for q in range(4):
-                nc.sync.dma_start(out=plane[32 * q : 32 * q + 4, :].bitcast(I32), in_=rows[0, 4 * q : 4 * q + 4, :].bitcast(I32))
-
         def pair(i, name):
             return psum.tile([P, 2 * BANK], F32, name=name, tag="pair%d" % i)
 
+        def load_scales(plane, scale_rows):
+            for q in range(4):
+                nc.sync.dma_start(
+                    out=plane[32 * q : 32 * q + 4, :].bitcast(I32),
+                    in_=scale_rows[0, 4 * q : 4 * q + 4, :].bitcast(I32),
+                )
+
         xb_rows = xb.rearrange("(p r) j -> p r j", r=PACK)
-        raw_head = pages.tile([P, PACK, 2 * T // PACK], F32, name="raw_head", offset=2 * 4 * T)
+        raw_head = pages.tile([P, PACK, T // PACK], F32, name="raw_head", offset=PAGE_BYTES * (TILES + LAST))
         raw_rest = sb.tile([P, PACK, REST], F32, name="raw_rest")
         wb_codes = sb.tile([P, 2 * N], U8, name="wb_codes", align_bytes=64)
         wb_plane = sb.tile([P, N], U8, name="wb_plane", align_bytes=64)
@@ -54,17 +62,17 @@ def tile_list_weighted_writes_kernel(tc, xa_words, xa_scales, wa_words, wa_scale
         xa_plane = sb.tile([P, J], U8, name="xa_plane", align_bytes=64)
         wa_codes = sb.tile([P, N], U32, name="wa_codes", align_bytes=64)
         wa_plane = sb.tile([P, N], U8, name="wa_plane", align_bytes=64)
-        offsets = sb.tile([P, J // 16], U16, name="offsets")
+        offsets = sb.tile([P, J // GROUP], U16, name="offsets")
 
         nc.sync.dma_start(out=raw_head[:, :, 0:HEAD], in_=xb_rows[:, :, 0:HEAD])
         load_scales(wb_plane, wb_scales)
         nc.sync.dma_start(out=wb_codes[:].bitcast(I32), in_=wb_words[0].bitcast(I32))
         nc.sync.dma_start(out=raw_rest[:], in_=xb_rows[:, :, HEAD:J])
-        nc.sync.dma_start(offsets[:], offs)
+        nc.sync.dma_start(out=xa_codes[:].bitcast(I32), in_=xa_words[0].bitcast(I32))
         load_scales(wa_plane, wa_scales)
         load_scales(xa_plane, xa_scales)
-        nc.sync.dma_start(out=xa_codes[:].bitcast(I32), in_=xa_words[0].bitcast(I32))
         nc.sync.dma_start(out=wa_codes[:].bitcast(I32), in_=wa_words[0].rearrange("p n r -> p (n r)").bitcast(I32))
+        nc.sync.dma_start(offsets[:], offs)
         prior, state = [], []
         for t in range(TILES):
             prior.append(sb.tile([P, T], F32, name="prior%d" % t))
@@ -111,23 +119,27 @@ def tile_list_weighted_writes_kernel(tc, xa_words, xa_scales, wa_words, wa_scale
                 stop=True,
             )
 
+        def by_tile(ap):
+            return ap.rearrange("p (t j) -> p t j", t=TILES)
+
         room_head = sb.tile([P, HEAD * PACK], BF16, name="room_head", align_bytes=64)
         quantise(interleave(raw_head, 0, HEAD, room_head), 0, HEAD)
         u_head = bank(0, "u_head")
         for t in range(TILES):
             product_u(u_head[:, HEAD * t : HEAD * (t + 1)], t, 0, HEAD)
-        decay = sb.tile([P, TILES, REST], F32, name="decay")
+        gate = sb.tile([P, TILES, REST], F32, name="gate")
         log_head = sb.tile([P, TILES, HEAD], F32, name="log_head")
-        nc.scalar.activation(decay[:, :, 0:HEAD], u_head[:].rearrange("p (t j) -> p t j", t=TILES), ACT.Sigmoid, scale=-1.0)
-        nc.scalar.activation(log_head[:], decay[:, :, 0:HEAD], ACT.Ln, bias=TINY)
+        nc.scalar.activation(gate[:, :, 0:HEAD], by_tile(u_head[:]), ACT.Sigmoid, scale=-1.0)
+        for t in range(0, TILES, 2):
+            nc.scalar.activation(log_head[:, t : t + 2, :], gate[:, t : t + 2, 0:HEAD], ACT.Ln, bias=TINY)
 
         rooms = [
             sb.tile([P, HEAD * PACK], BF16, name="room_first", align_bytes=64),
-            pages.tile([P, 2 * TILES * T], BF16, name="room_last", align_bytes=64, offset=4 * T * TILES),
+            pages.tile([P, 5 * PAGE_BYTES // 2], BF16, name="room_last", align_bytes=64, offset=PAGE_BYTES * 2),
         ]
-        grouped = [interleave(raw_rest, lo, hi, room) for room, (lo, hi) in zip(rooms, REST_PARTS)]
-        for g, (lo, hi) in zip(grouped, REST_PARTS):
-            quantise(g, HEAD + lo, HEAD + hi)
+        grouped_rest = [interleave(raw_rest, lo, hi, room) for room, (lo, hi) in zip(rooms, REST_PARTS)]
+        for grouped, (lo, hi) in zip(grouped_rest, REST_PARTS):
+            quantise(grouped, HEAD + lo, HEAD + hi)
         u_pairs = [pair(i, "u_pair%d" % i) for i in range(2)]
         u_rest = [u_pairs[t // 2][:, BANK * (t % 2) : BANK * (t % 2 + 1)] for t in range(TILES)]
         for t in range(TILES):
@@ -139,76 +151,79 @@ def tile_list_weighted_writes_kernel(tc, xa_words, xa_scales, wa_words, wa_scale
 
         den, num = [], []
         for t in range(TILES):
-            den.append(pages.tile([P, T], F32, name="den%d" % t, offset=4 * T * t))
-            num.append(pages.tile([P, T], F32, name="num%d" % t, offset=4 * T * (TILES + t)))
-        for page in den:
+            den.append(pages.tile([P, T], F32, name="den%d" % t, offset=PAGE_BYTES * t))
+            num.append(pages.tile([P, T], F32, name="num%d" % t, offset=PAGE_BYTES * (TILES + t)))
+        for page in den[:2] + num[LAST:]:
             nc.vector.memset(page[:], 0.0)
-        for page in num:
+        for page in den[2:] + num[:LAST]:
             nc.gpsimd.memset(page[:], 0.0)
 
         s_head = sb.tile([P, TILES * HEAD], F32, name="s_head")
         sv = sb.tile([P, TILES, J], F32, name="sv")
-        nc.vector.scalar_tensor_tensor(s_head[:], log_head[:].rearrange("p t j -> p (t j)"), -1.0, u_head[:], ALU.mult, ALU.max)
-        head_list = offsets[:, 0 : HEAD // 16]
+        for t in range(0, TILES, 2):
+            cols = slice(HEAD * t, HEAD * (t + 2))
+            logs = log_head[:].rearrange("p t j -> p (t j)")[:, cols]
+            nc.vector.scalar_tensor_tensor(s_head[:, cols], logs, -1.0, u_head[:, cols], ALU.mult, ALU.max)
+        head_list = offsets[:, 0 : HEAD // GROUP]
         for t in range(TILES):
             nc.vector.tensor_copy(den[t][:].indirect(head_list), s_head[:, HEAD * t : HEAD * (t + 1)])
-        nc.vector.tensor_tensor(sv[:, :, 0:HEAD], s_head[:].rearrange("p (t j) -> p t j", t=TILES), v_head[:].rearrange("p (t j) -> p t j", t=TILES), ALU.mult)
-        for t in range(TILES - 1):
+        nc.vector.tensor_tensor(sv[:, :, 0:HEAD], by_tile(s_head[:]), by_tile(v_head[:]), ALU.mult)
+        for t in range(LAST):
             nc.vector.tensor_copy(num[t][:].indirect(head_list), sv[:, t, 0:HEAD])
 
         v_rest = [bank(b, "v_rest%d" % b) for b in (2, 3, 0, 1)]
         for t in range(TILES):
             for lo, hi in REST_PARTS:
                 product_v(v_rest[t][:, lo:hi], t, HEAD + lo, HEAD + hi)
-
         for t in range(TILES):
-            nc.scalar.activation(decay[:, t, :], u_rest[t][:, 0:REST], ACT.Sigmoid, scale=-1.0)
-        nc.scalar.activation(decay[:], decay[:], ACT.Ln, bias=TINY)
-
+            nc.scalar.activation(gate[:, t, :], u_rest[t][:, 0:REST], ACT.Sigmoid, scale=-1.0)
+        for t in range(0, TILES, 2):
+            nc.scalar.activation(gate[:, t : t + 2, :], gate[:, t : t + 2, :], ACT.Ln, bias=TINY)
         weighted = [sb.tile([P, T], F32, name="weighted%d" % t) for t in range(TILES)]
         for t in range(TILES):
             nc.gpsimd.tensor_tensor(weighted[t][:], prior[t][:], state[t][:], ALU.mult)
 
-        rest_list = offsets[:, HEAD // 16 : J // 16]
+        rest_list = offsets[:, HEAD // GROUP : J // GROUP]
         s_rest = [sb.tile([P, REST], F32, name="s_rest%d" % t) for t in range(TILES)]
         for t in range(TILES):
-            nc.vector.scalar_tensor_tensor(s_rest[t][:], decay[:, t, :], -1.0, u_rest[t][:, 0:REST], ALU.mult, ALU.max)
+            nc.vector.scalar_tensor_tensor(s_rest[t][:], gate[:, t, :], -1.0, u_rest[t][:, 0:REST], ALU.mult, ALU.max)
+
+        halves = [slice(BANK * h, BANK * (h + 1)) for h in range(T // BANK)]
+        blocks = [[slice(c, c + P) for c in range(half.start, half.stop, P)] for half in halves]
         for t in range(TILES):
             nc.vector.tensor_tensor(sv[:, t, HEAD:J], s_rest[t][:], v_rest[t][:, 0:REST], ALU.mult)
             nc.vector.tensor_copy(den[t][:].indirect(rest_list), s_rest[t][:])
-            if t < TILES - 1:
+            if t < LAST:
                 nc.vector.tensor_copy(num[t][:].indirect(rest_list), sv[:, t, HEAD:J])
             else:
                 nc.vector.tensor_copy(num[t][:].indirect(offsets[:]), sv[:, t, :])
 
             recip = sb.tile([P, T], F32, name="recip%d" % t)
-            halves = [slice(BANK * h, BANK * (h + 1)) for h in range(2)]
-            blocks = [[slice(BANK * h + P * k, BANK * h + P * (k + 1)) for k in range(BANK // P)] for h in range(2)]
             total = pair(0, "total")
-            for h in range(2):
-                for k, cols in enumerate(blocks[h]):
-                    nc.tensor.matmul(total[:, cols], prior[t][:, cols], ident[:], start=(k == 0), stop=False, is_transpose=True)
+            for in_bank in blocks:
+                for cols in in_bank:
+                    nc.tensor.matmul(total[:, cols], prior[t][:, cols], ident[:], start=(cols == in_bank[0]), stop=False, is_transpose=True)
             root = ring.tile([P, T], F32, name="root")
-            for h in range(2):
-                for k, cols in enumerate(blocks[h]):
-                    nc.tensor.matmul(total[:, cols], den[t][:, cols], ident[:], start=False, stop=(k == len(blocks[h]) - 1), is_transpose=True)
-                nc.scalar.activation(root[:, halves[h]], total[:, halves[h]], ACT.Abs_reciprocal_sqrt)
+            for half, in_bank in zip(halves, blocks):
+                for cols in in_bank:
+                    nc.tensor.matmul(total[:, cols], den[t][:, cols], ident[:], start=False, stop=(cols == in_bank[-1]), is_transpose=True)
+                nc.scalar.activation(root[:, half], total[:, half], ACT.Abs_reciprocal_sqrt)
             back = pair(1, "back")
-            for h in range(2):
-                for cols in blocks[h]:
+            for half, in_bank in zip(halves, blocks):
+                for cols in in_bank:
                     nc.tensor.transpose(back[:, cols], root[:, cols], ident[:])
-                nc.scalar.activation(recip[:, halves[h]], back[:, halves[h]], ACT.Square)
+                nc.scalar.activation(recip[:, half], back[:, half], ACT.Square)
 
             rows = slice(P * t, P * (t + 1))
             result = ring.tile([P, T], F32, name="result")
-            if t < TILES - 1:
-                summed = sb.tile([P, T], F32, name="summed", tag="state%d" % (TILES - 1))
+            if t < LAST:
+                summed = sb.tile([P, T], F32, name="summed", tag="state%d" % LAST)
                 nc.gpsimd.tensor_tensor(summed[:], num[t][:], weighted[t][:], ALU.add)
                 nc.gpsimd.tensor_tensor(result[:], summed[:], recip[:], ALU.mult)
                 nc.sync.dma_start(out=out[rows, :], in_=result[:])
             else:
-                for cols in halves:
-                    nc.vector.tensor_tensor(weighted[t][:, cols], num[t][:, cols], weighted[t][:, cols], ALU.add)
-                for cols in halves:
-                    nc.vector.tensor_tensor(result[:, cols], weighted[t][:, cols], recip[:, cols], ALU.mult)
-                    nc.sync.dma_start(out=out[rows, cols], in_=result[:, cols])
+                for half in halves:
+                    nc.vector.tensor_tensor(weighted[t][:, half], num[t][:, half], weighted[t][:, half], ALU.add)
+                for half in halves:
+                    nc.vector.tensor_tensor(result[:, half], weighted[t][:, half], recip[:, half], ALU.mult)
+                    nc.sync.dma_start(out=out[rows, half], in_=result[:, half])

from contextlib import ExitStack

import concourse.mybir as mybir
from concourse.masks import make_identity

K, L, T, J, N = 512, 512, 1024, 512, 512
FLOPS = 2 * K * N * J + 2 * L * N * J

F32 = mybir.dt.float32
BF16 = mybir.dt.bfloat16
I32 = mybir.dt.int32
U32 = mybir.dt.uint32
U16 = mybir.dt.uint16
U8 = mybir.dt.uint8
FP8X4 = mybir.dt.float8_e4m3fn_x4
FP4X4 = mybir.dt.float4_e2m1fn_x4
ACT = mybir.ActivationFunctionType
ALU = mybir.AluOpType

P = 128
PACK = 4
TILES = N // P
LAST = TILES - 1
BANK = 512
PAGE_BYTES = 4 * T
GROUP = 16

HEAD = 128
REST = J - HEAD
REST_PARTS = ((0, 128), (128, 384))

TINY = 2.0**-60


def tile_list_weighted_writes_kernel(tc, xa_words, xa_scales, wa_words, wa_scales, xb, wb_words, wb_scales, pr, old, offs, out):
    nc = tc.nc
    with ExitStack() as ctx:
        sb = ctx.enter_context(tc.tile_pool(name="sb", bufs=1))
        ring = ctx.enter_context(tc.tile_pool(name="ring", bufs=2))
        pages = ctx.enter_context(tc.tile_pool(name="pages", bufs=1))
        psum = ctx.enter_context(tc.psum_pool(name="psum", bufs=1))

        def bank(i, name):
            return psum.tile([P, BANK], F32, name=name, tag="bank%d" % i)

        def pair(i, name):
            return psum.tile([P, 2 * BANK], F32, name=name, tag="pair%d" % i)

        def load_scales(plane, scale_rows):
            for q in range(4):
                nc.sync.dma_start(
                    out=plane[32 * q : 32 * q + 4, :].bitcast(I32),
                    in_=scale_rows[0, 4 * q : 4 * q + 4, :].bitcast(I32),
                )

        xb_rows = xb.rearrange("(p r) j -> p r j", r=PACK)
        raw_head = pages.tile([P, PACK, T // PACK], F32, name="raw_head", offset=PAGE_BYTES * (TILES + LAST))
        raw_rest = sb.tile([P, PACK, REST], F32, name="raw_rest")
        wb_codes = sb.tile([P, 2 * N], U8, name="wb_codes", align_bytes=64)
        wb_plane = sb.tile([P, N], U8, name="wb_plane", align_bytes=64)
        xa_codes = sb.tile([P, 2 * J], U8, name="xa_codes", align_bytes=64)
        xa_plane = sb.tile([P, J], U8, name="xa_plane", align_bytes=64)
        wa_codes = sb.tile([P, N], U32, name="wa_codes", align_bytes=64)
        wa_plane = sb.tile([P, N], U8, name="wa_plane", align_bytes=64)
        offsets = sb.tile([P, J // GROUP], U16, name="offsets")

        nc.sync.dma_start(out=raw_head[:, :, 0:HEAD], in_=xb_rows[:, :, 0:HEAD])
        load_scales(wb_plane, wb_scales)
        nc.sync.dma_start(out=wb_codes[:].bitcast(I32), in_=wb_words[0].bitcast(I32))
        nc.sync.dma_start(out=raw_rest[:], in_=xb_rows[:, :, HEAD:J])
        nc.sync.dma_start(out=xa_codes[:].bitcast(I32), in_=xa_words[0].bitcast(I32))
        load_scales(wa_plane, wa_scales)
        load_scales(xa_plane, xa_scales)
        nc.sync.dma_start(out=wa_codes[:].bitcast(I32), in_=wa_words[0].rearrange("p n r -> p (n r)").bitcast(I32))
        nc.sync.dma_start(offsets[:], offs)
        prior, state = [], []
        for t in range(TILES):
            prior.append(sb.tile([P, T], F32, name="prior%d" % t))
            state.append(sb.tile([P, T], F32, name="state%d" % t, tag="state%d" % t))
            nc.sync.dma_start(out=prior[t][:], in_=pr[P * t : P * (t + 1), :])
            nc.sync.dma_start(out=state[t][:], in_=old[P * t : P * (t + 1), :])

        ident = sb.tile([P, P], F32, name="ident")
        make_identity(nc, ident[:])

        xb_codes = sb.tile([P, J], U32, name="xb_codes", align_bytes=64)
        xb_plane = sb.tile([P, J], U8, name="xb_plane", align_bytes=64)

        def interleave(raw, lo, hi, room):
            grouped = room[:, 0 : (hi - lo) * PACK]
            nc.vector.tensor_copy(
                out=grouped.rearrange("p (c i r) -> p c r i", i=4, r=PACK),
                in_=raw[:, :, lo:hi].rearrange("p r (c i) -> p c r i", i=4),
            )
            return grouped

        def quantise(grouped, j0, j1):
            nc.vector.quantize_mx(out=xb_codes[:, j0:j1].bitcast(FP8X4), scales=xb_plane[:, j0:j1], in_=grouped)

        def product_u(dst, t, j0, j1):
            nc.tensor.matmul_mx(
                dst,
                lhsT=wb_codes[:, 2 * P * t : 2 * P * (t + 1)].bitcast(FP4X4),
                lhsT_scale=wb_plane[:, P * t : P * (t + 1)],
                rhs=xb_codes[:, j0:j1].bitcast(FP8X4),
                rhs_scale=xb_plane[:, j0:j1],
                start=True,
                stop=True,
            )

        def product_v(dst, t, j0, j1):
            nc.tensor.matmul_mx(
                dst,
                lhsT=wa_codes[:, P * t : P * (t + 1)].bitcast(FP8X4),
                lhsT_scale=wa_plane[:, P * t : P * (t + 1)],
                rhs=xa_codes[:, 2 * j0 : 2 * j1].bitcast(FP4X4),
                rhs_scale=xa_plane[:, j0:j1],
                start=True,
                stop=True,
            )

        def by_tile(ap):
            return ap.rearrange("p (t j) -> p t j", t=TILES)

        room_head = sb.tile([P, HEAD * PACK], BF16, name="room_head", align_bytes=64)
        quantise(interleave(raw_head, 0, HEAD, room_head), 0, HEAD)
        u_head = bank(0, "u_head")
        for t in range(TILES):
            product_u(u_head[:, HEAD * t : HEAD * (t + 1)], t, 0, HEAD)
        gate = sb.tile([P, TILES, REST], F32, name="gate")
        log_head = sb.tile([P, TILES, HEAD], F32, name="log_head")
        nc.scalar.activation(gate[:, :, 0:HEAD], by_tile(u_head[:]), ACT.Sigmoid, scale=-1.0)
        for t in range(0, TILES, 2):
            nc.scalar.activation(log_head[:, t : t + 2, :], gate[:, t : t + 2, 0:HEAD], ACT.Ln, bias=TINY)

        rooms = [
            sb.tile([P, HEAD * PACK], BF16, name="room_first", align_bytes=64),
            pages.tile([P, 5 * PAGE_BYTES // 2], BF16, name="room_last", align_bytes=64, offset=PAGE_BYTES * 2),
        ]
        grouped_rest = [interleave(raw_rest, lo, hi, room) for room, (lo, hi) in zip(rooms, REST_PARTS)]
        for grouped, (lo, hi) in zip(grouped_rest, REST_PARTS):
            quantise(grouped, HEAD + lo, HEAD + hi)
        u_pairs = [pair(i, "u_pair%d" % i) for i in range(2)]
        u_rest = [u_pairs[t // 2][:, BANK * (t % 2) : BANK * (t % 2 + 1)] for t in range(TILES)]
        for t in range(TILES):
            for lo, hi in REST_PARTS:
                product_u(u_rest[t][:, lo:hi], t, HEAD + lo, HEAD + hi)
        v_head = bank(1, "v_head")
        for t in range(TILES):
            product_v(v_head[:, HEAD * t : HEAD * (t + 1)], t, 0, HEAD)

        den, num = [], []
        for t in range(TILES):
            den.append(pages.tile([P, T], F32, name="den%d" % t, offset=PAGE_BYTES * t))
            num.append(pages.tile([P, T], F32, name="num%d" % t, offset=PAGE_BYTES * (TILES + t)))
        for page in den[:2] + num[LAST:]:
            nc.vector.memset(page[:], 0.0)
        for page in den[2:] + num[:LAST]:
            nc.gpsimd.memset(page[:], 0.0)

        s_head = sb.tile([P, TILES * HEAD], F32, name="s_head")
        sv = sb.tile([P, TILES, J], F32, name="sv")
        for t in range(0, TILES, 2):
            cols = slice(HEAD * t, HEAD * (t + 2))
            logs = log_head[:].rearrange("p t j -> p (t j)")[:, cols]
            nc.vector.scalar_tensor_tensor(s_head[:, cols], logs, -1.0, u_head[:, cols], ALU.mult, ALU.max)
        head_list = offsets[:, 0 : HEAD // GROUP]
        for t in range(TILES):
            nc.vector.tensor_copy(den[t][:].indirect(head_list), s_head[:, HEAD * t : HEAD * (t + 1)])
        nc.vector.tensor_tensor(sv[:, :, 0:HEAD], by_tile(s_head[:]), by_tile(v_head[:]), ALU.mult)
        for t in range(LAST):
            nc.vector.tensor_copy(num[t][:].indirect(head_list), sv[:, t, 0:HEAD])

        v_rest = [bank(b, "v_rest%d" % b) for b in (2, 3, 0, 1)]
        for t in range(TILES):
            for lo, hi in REST_PARTS:
                product_v(v_rest[t][:, lo:hi], t, HEAD + lo, HEAD + hi)
        for t in range(TILES):
            nc.scalar.activation(gate[:, t, :], u_rest[t][:, 0:REST], ACT.Sigmoid, scale=-1.0)
        for t in range(0, TILES, 2):
            nc.scalar.activation(gate[:, t : t + 2, :], gate[:, t : t + 2, :], ACT.Ln, bias=TINY)
        weighted = [sb.tile([P, T], F32, name="weighted%d" % t) for t in range(TILES)]
        for t in range(TILES):
            nc.gpsimd.tensor_tensor(weighted[t][:], prior[t][:], state[t][:], ALU.mult)

        rest_list = offsets[:, HEAD // GROUP : J // GROUP]
        s_rest = [sb.tile([P, REST], F32, name="s_rest%d" % t) for t in range(TILES)]
        for t in range(TILES):
            nc.vector.scalar_tensor_tensor(s_rest[t][:], gate[:, t, :], -1.0, u_rest[t][:, 0:REST], ALU.mult, ALU.max)

        halves = [slice(BANK * h, BANK * (h + 1)) for h in range(T // BANK)]
        blocks = [[slice(c, c + P) for c in range(half.start, half.stop, P)] for half in halves]
        for t in range(TILES):
            nc.vector.tensor_tensor(sv[:, t, HEAD:J], s_rest[t][:], v_rest[t][:, 0:REST], ALU.mult)
            nc.vector.tensor_copy(den[t][:].indirect(rest_list), s_rest[t][:])
            if t < LAST:
                nc.vector.tensor_copy(num[t][:].indirect(rest_list), sv[:, t, HEAD:J])
            else:
                nc.vector.tensor_copy(num[t][:].indirect(offsets[:]), sv[:, t, :])

            recip = sb.tile([P, T], F32, name="recip%d" % t)
            total = pair(0, "total")
            for in_bank in blocks:
                for cols in in_bank:
                    nc.tensor.matmul(total[:, cols], prior[t][:, cols], ident[:], start=(cols == in_bank[0]), stop=False, is_transpose=True)
            root = ring.tile([P, T], F32, name="root")
            for half, in_bank in zip(halves, blocks):
                for cols in in_bank:
                    nc.tensor.matmul(total[:, cols], den[t][:, cols], ident[:], start=False, stop=(cols == in_bank[-1]), is_transpose=True)
                nc.scalar.activation(root[:, half], total[:, half], ACT.Abs_reciprocal_sqrt)
            back = pair(1, "back")
            for half, in_bank in zip(halves, blocks):
                for cols in in_bank:
                    nc.tensor.transpose(back[:, cols], root[:, cols], ident[:])
                nc.scalar.activation(recip[:, half], back[:, half], ACT.Square)

            rows = slice(P * t, P * (t + 1))
            result = ring.tile([P, T], F32, name="result")
            if t < LAST:
                summed = sb.tile([P, T], F32, name="summed", tag="state%d" % LAST)
                nc.gpsimd.tensor_tensor(summed[:], num[t][:], weighted[t][:], ALU.add)
                nc.gpsimd.tensor_tensor(result[:], summed[:], recip[:], ALU.mult)
                nc.sync.dma_start(out=out[rows, :], in_=result[:])
            else:
                for half in halves:
                    nc.vector.tensor_tensor(weighted[t][:, half], num[t][:, half], weighted[t][:, half], ALU.add)
                for half in halves:
                    nc.vector.tensor_tensor(result[:, half], weighted[t][:, half], recip[:, half], ALU.mult)
                    nc.sync.dma_start(out=out[rows, half], in_=result[:, half])
